import numpy as np
import ml_dtypes


def mxq(x, axis, fmt="e4m3"):
    dtype, down = {"e4m3": (ml_dtypes.float8_e4m3fn, 7), "e5m2": (ml_dtypes.float8_e5m2, 14)}[fmt]
    v = np.moveaxis(np.asarray(x, np.float32).astype(ml_dtypes.bfloat16).astype(np.float64), axis, -1)
    blocks = v.reshape(v.shape[:-1] + (-1, 32))
    amax = np.abs(blocks).max(-1, keepdims=True)
    byte = np.maximum(np.where(amax > 0, np.frexp(amax)[1] - 1 + 127, 0) - down, 1)
    scale = np.exp2(byte - 127.0)
    codes = (blocks / scale).astype(np.float32).astype(dtype).astype(np.float64)
    return np.moveaxis((codes * scale).reshape(v.shape), -1, axis)


WIDE = False


def mx_kscale(k):
    if not WIDE:
        return np.ones(k)
    levels = np.array([10, -10, 5, -5, 0])
    if k % 512:
        return np.exp2(np.random.permutation(np.resize(levels, k // 32))).repeat(32)
    a = np.empty((k // 512, 16))
    for p in range(k // 512):
        a[p, :8] = np.random.permutation(np.resize(levels, 8))
        for g in range(8):
            far = levels[np.abs(levels - a[p, g]) >= 10]
            a[p, g + 8] = far[np.random.randint(len(far))]
    return np.exp2(a.ravel()).repeat(32)


BF16 = ml_dtypes.bfloat16


def bf(x):
    return np.asarray(x, np.float32).astype(BF16)


def f64(x):
    return np.asarray(x).astype(np.float64)


E2M1 = np.array([0.0, 0.5, 1.0, 1.5, 2.0, 3.0, 4.0, 6.0, -0.0, -0.5, -1.0, -1.5, -2.0, -3.0, -4.0, -6.0])


def pack_weight(w, fmt):
    k, n = w.shape
    w = f64(bf(w)).reshape(k // 32, 32, n)
    amax = np.abs(w).max(1)
    if fmt == "e4m3":
        byte = np.frexp(amax)[1] - 1 + 127 - 7
    else:
        mant, ex = np.frexp(amax / 6.0)
        byte = np.where(mant > 0.5, ex, ex - 1) + 127
    byte = np.clip(np.where(amax > 0, byte, 1), 1, 254)
    scaled = (w * np.exp2(127.0 - byte)[:, None, :]).reshape(k, n).astype(np.float32)
    by_word = np.ascontiguousarray(scaled.reshape(k // 512, 128, 4, n).transpose(0, 1, 3, 2))
    if fmt == "e4m3":
        words = by_word.astype(ml_dtypes.float8_e4m3fn).view(np.uint8)
    else:
        c = by_word.astype(ml_dtypes.float4_e2m1fn).view(np.uint8) & 0xF
        words = c[..., 0::2] | (c[..., 1::2] << 4)
    return np.ascontiguousarray(words), np.ascontiguousarray(byte.astype(np.uint8).reshape(k // 512, 16, n))


def unpack_weight(words, scales, fmt):
    g, p, n, _ = words.shape
    if fmt == "e4m3":
        vals = np.ascontiguousarray(words).view(ml_dtypes.float8_e4m3fn).astype(np.float64)
    else:
        nib = np.empty((g, p, n, 4), np.uint8)
        nib[..., 0::2] = words & 0xF
        nib[..., 1::2] = words >> 4
        vals = E2M1[nib]
    vals = vals * np.repeat(np.exp2(scales.astype(np.float64) - 127.0), 8, axis=1)[..., None]
    return vals.transpose(0, 1, 3, 2).reshape(g * 512, n)

def planes(Y):
    n, m = Y.shape
    b = f64(bf(Y)).reshape(n // 32, 32, m)
    amax = np.abs(b).max(1)
    byte = np.clip(np.where(amax > 0, np.frexp(amax)[1] - 1 + 127 - 7, 1), 1, 254)
    codes = (b * np.exp2(127.0 - byte)[:, None, :]).reshape(n, m).astype(np.float32).astype(ml_dtypes.float8_e4m3fn).view(np.uint8)
    words = codes.reshape(n // 512, 128, 4, m).transpose(0, 1, 3, 2)
    return np.ascontiguousarray(words), np.ascontiguousarray(byte.astype(np.uint8).reshape(n // 512, 16, m))


B, S, D = 2, 512, 512
TWO = 2


def softmax_last(logit):
    top = np.max(logit, axis=-1, keepdims=True)
    e = np.exp(logit - top)
    return e / np.sum(e, axis=-1, keepdims=True)


def setup_inputs():
    s, t = mx_kscale(D), mx_kscale(S)
    x = bf(np.random.standard_normal((B, S, D)) * s)
    w_words, w_scales = pack_weight(np.random.standard_normal((D, S)) * (2.0 / np.sqrt(D)) / s[:, None], "e4m3")
    rnd = bf(np.random.standard_normal((S, S)) * 1.5)
    mix = bf(np.random.uniform(0.5, 0.9, (TWO,)))
    wv_words, wv_scales = pack_weight(np.random.standard_normal((D, D)) / np.sqrt(D) / s[:, None], "e4m3")
    c = bf(np.random.standard_normal(S) * (0.25 * np.sqrt(S)) * t)
    u = bf((1.0 + 0.1 * np.random.standard_normal(S)) / t)
    return {"x": x, "w_words": w_words, "w_scales": w_scales, "rnd": rnd, "mix": mix, "wv_words": wv_words, "wv_scales": wv_scales, "c": c, "u": u}


def core(x, w_words, w_scales, rnd, mix, wv_words, wv_scales, c, u):
    mix = f64(mix)
    xq = mxq(f64(x), 2, "e4m3")
    syn = xq @ unpack_weight(w_words, w_scales, "e4m3")
    logit = mix[0] * syn + mix[1] * f64(rnd)[None, :, :]
    p = softmax_last(logit)
    pc = p * f64(c)[None, None, :]
    v = f64(u)[None, :, None] * (xq @ unpack_weight(wv_words, wv_scales, "e4m3"))
    return mxq(pc, 2, "e4m3") @ mxq(v, 1, "e4m3")


def reference(x, w_words, w_scales, rnd, mix, wv_words, wv_scales, c, u):
    R_out = core(x, w_words, w_scales, rnd, mix, wv_words, wv_scales, c, u)
    words, scales = planes(np.moveaxis(R_out, 2, 0).reshape(512, -1))
    return R_out, words, scales

@@ -1,0 +1,357 @@
+from contextlib import ExitStack
+
+import concourse.mybir as mybir
+from concourse.masks import make_identity
+
+B, S, D = 2, 512, 512
+FLOPS = 3 * 2 * B * S * S * D
+
+F32 = mybir.dt.float32
+BF16 = mybir.dt.bfloat16
+U32 = mybir.dt.uint32
+I32 = mybir.dt.int32
+U8 = mybir.dt.uint8
+X4 = mybir.dt.float8_e4m3fn_x4
+ALU = mybir.AluOpType
+ACT = mybir.ActivationFunctionType
+AXIS = mybir.AxisListType
+
+P = 128
+PACK = 4
+TILES = S // P
+N_TILES = B * TILES
+MANUAL_ORDER = True
+
+
+def tile_mixturedenserandomsynthesizer_x2_kernel(
+    tc, x, w_words, w_scales, rnd, mix, wv_words, wv_scales, c, u, out_0, out_1, out_2
+):
+    nc = tc.nc
+    with ExitStack() as ctx:
+        keep = ctx.enter_context(tc.tile_pool(name="keep", bufs=1))
+        work = ctx.enter_context(tc.tile_pool(name="work", bufs=4))
+        psum = ctx.enter_context(tc.psum_pool(name="psum", bufs=2))
+
+        x_sb = [keep.tile([P, TILES, D], BF16, name="x_sb%d" % b) for b in range(B)]
+        w_sb = keep.tile([P, S], U32, name="w_sb", align_bytes=64)
+        wv_sb = keep.tile([P, D], U32, name="wv_sb", align_bytes=64)
+        ws_sb = keep.tile([P, S], U8, name="ws_sb", align_bytes=64)
+        wvs_sb = keep.tile([P, D], U8, name="wvs_sb", align_bytes=64)
+        rnd_sb = keep.tile([P, TILES, S], BF16, name="rnd_sb")
+        rm = keep.tile([P, TILES, S], F32, name="rm")
+        mix_bf = keep.tile([P, 2], BF16, name="mix_bf")
+        u_bf = keep.tile([P, TILES], BF16, name="u_bf")
+        c_row = keep.tile([P, S], BF16, name="c_row")
+        ones = keep.tile([P, P], BF16, name="ones")
+        ident = keep.tile([P, P], F32, name="ident")
+        warm = keep.tile([P, 1], F32, name="warm")
+
+        x_v = [x[b].rearrange("(p t) f -> p t f", t=TILES) for b in range(B)]
+        rnd_v = rnd.rearrange("(p t) k -> p t k", t=TILES)
+
+        make_identity(nc, ident[:])
+        nc.gpsimd.dma_start(out=mix_bf[:], in_=mix.partition_broadcast(P))
+        nc.vector.memset(ws_sb[:].bitcast(I32), 0)
+        nc.vector.memset(wvs_sb[:].bitcast(I32), 0)
+        nc.vector.memset(warm[:], 0.0)
+        nc.vector.memset(c_row[:], 0.0)
+        nc.vector.memset(ones[:], 1.0)
+
+        def load_scales(eng, dst, src):
+            for q in range(4):
+                eng.dma_start(
+                    out=dst[32 * q : 32 * q + 4, :].bitcast(I32),
+                    in_=src[0, 4 * q : 4 * q + 4, :].bitcast(I32),
+                )
+
+        nc.sync.dma_start(out=x_sb[0][:, 0:1, :], in_=x_v[0][:, 0:1, :])
+        nc.sync.dma_start(
+            out=w_sb[:].bitcast(I32), in_=w_words[0].rearrange("p n t -> p (n t)").bitcast(I32)
+        )
+        load_scales(nc.scalar, ws_sb, w_scales)
+        nc.scalar.activation(out=warm[:], in_=warm[:], func=ACT.Exp)
+        nc.sync.dma_start(out=rnd_sb[:, 0:2, :], in_=rnd_v[:, 0:2, :])
+        nc.sync.dma_start(out=x_sb[0][:, 1:4, :], in_=x_v[0][:, 1:4, :])
+        nc.gpsimd.dma_start(out=c_row[0:1, :], in_=c.rearrange("(o k) -> o k", o=1))
+        nc.gpsimd.dma_start(out=u_bf[:], in_=u.rearrange("(p t) -> p t", t=TILES))
+        nc.sync.dma_start(
+            out=wv_sb[:].bitcast(I32), in_=wv_words[0].rearrange("p n t -> p (n t)").bitcast(I32)
+        )
+        load_scales(nc.sync, wvs_sb, wv_scales)
+        nc.sync.dma_start(out=rnd_sb[:, 2:4, :], in_=rnd_v[:, 2:4, :])
+        nc.sync.dma_start(out=x_sb[1][:], in_=x_v[1])
+
+        c_ps = psum.tile([P, S], F32, name="c_ps", bufs=1)
+
+        def rnd_mix(t):
+            (nc.vector if t == 0 else nc.gpsimd).tensor_scalar(
+                out=rm[:, t, :], in0=rnd_sb[:, t, :], scalar1=mix_bf[:, 1:2], scalar2=0.0,
+                op0=ALU.mult, op1=ALU.add,
+            )
+
+        xq = [keep.tile([P, S], U32, name="xq%d" % b, align_bytes=64) for b in range(B)]
+        xs = [keep.tile([P, S], U8, name="xs%d" % b, align_bytes=64) for b in range(B)]
+        vg = [keep.tile([P, D, PACK], BF16, name="vg%d" % b, align_bytes=64) for b in range(B)]
+        vq = [keep.tile([P, D], U32, name="vq%d" % b, align_bytes=64) for b in range(B)]
+        vs = [keep.tile([P, D], U8, name="vs%d" % b, align_bytes=64) for b in range(B)]
+        og = [keep.tile([P, S, PACK], BF16, name="og%d" % b, align_bytes=64) for b in range(B)]
+        oq = [keep.tile([P, S], U32, name="oq%d" % b, align_bytes=64) for b in range(B)]
+        os_ = [keep.tile([P, S], U8, name="os%d" % b, align_bytes=64) for b in range(B)]
+
+        state = {}
+
+        def x_turn(n):
+            b, t = divmod(n, TILES)
+            words = x_sb[b][:, t, :].bitcast(F32)
+            xt = psum.tile([P, 2, P], F32, name="turn")
+            for h in range(2):
+                nc.tensor.transpose(xt[:, h, :], words[:, h : 2 * P : 2], ident[:])
+            xg = work.tile([P, P, PACK], BF16, name="xg", align_bytes=64)
+            nc.scalar.copy(
+                out=xg[:].rearrange("p n j -> p (n j)").bitcast(F32).rearrange("p (n h) -> p n h", h=2),
+                in_=xt[:].rearrange("p h n -> p n h"),
+            )
+            state["xg", n] = xg
+
+        def x_quant(n):
+            b, t = divmod(n, TILES)
+            cols = slice(P * t, P * (t + 1))
+            nc.vector.quantize_mx(
+                out=xq[b][:, cols].bitcast(X4), scales=xs[b][:, cols],
+                in_=state["xg", n][:].rearrange("p n j -> p (n j)"),
+            )
+
+        def syn(n):
+            b, t = divmod(n, TILES)
+            cols = slice(P * t, P * (t + 1))
+            ps = psum.tile([P, S], F32, name="syn_ps")
+            nc.tensor.matmul_mx(
+                out=ps[:], lhsT=xq[b][:, cols].bitcast(X4), lhsT_scale=xs[b][:, cols],
+                rhs=w_sb[:].bitcast(X4), rhs_scale=ws_sb[:], start=True, stop=True,
+            )
+            state["syn", n] = ps
+
+        def logit(n):
+            t = n % TILES
+            lg = work.tile([P, S], F32, name="lg")
+            nc.vector.scalar_tensor_tensor(
+                out=lg[:], in0=state["syn", n][:], scalar=mix_bf[:, 0:1], in1=rm[:, t, :],
+                op0=ALU.mult, op1=ALU.add,
+            )
+            state["lg", n] = lg
+
+        def row_max(n):
+            nmax = work.tile([P, 1], F32, name="nmax")
+            nc.vector.tensor_reduce(
+                out=nmax[:], in_=state["lg", n][:], axis=AXIS.X, op=ALU.max, negate=True
+            )
+            state["nmax", n] = nmax
+
+        def expo(n):
+            e = work.tile([P, S], F32, name="e")
+            tot = work.tile([P, 1], F32, name="tot")
+            nc.scalar.activation(
+                out=e[:], in_=state["lg", n][:], func=ACT.Exp, bias=state["nmax", n][:],
+                scale=1.0, accum_out=tot[:],
+            )
+            state["e", n], state["tot", n] = e, tot
+
+        def recip(n):
+            rinv = work.tile([P, 1], F32, name="rinv")
+            nc.vector.reciprocal(rinv[:], state["tot", n][:])
+            state["rinv", n] = rinv
+
+        def pc(n):
+            pcs = work.tile([P, S], BF16, name="pcs", align_bytes=64)
+            nc.vector.scalar_tensor_tensor(
+                out=pcs[:], in0=state["e", n][:], scalar=state["rinv", n][:], in1=c_ps[:],
+                op0=ALU.mult, op1=ALU.mult,
+            )
+            state["pcs", n] = pcs
+
+        def p_turn(n):
+            words = state["pcs", n][:].bitcast(F32)
+            pt = psum.tile([P, 2, P], F32, name="turn")
+            for h in range(2):
+                nc.tensor.transpose(pt[:, h, :], words[:, h : 2 * P : 2], ident[:])
+            state["pt", n] = pt
+
+        def p_evac(n):
+            pg = work.tile([P, P, PACK], BF16, name="pg", align_bytes=64)
+            nc.scalar.copy(
+                out=pg[:].rearrange("p n j -> p (n j)").bitcast(F32).rearrange("p (n h) -> p n h", h=2),
+                in_=state["pt", n][:].rearrange("p h n -> p n h"),
+            )
+            state["pg", n] = pg
+
+        def p_quant(n):
+            pq = work.tile([P, P], U32, name="pq", align_bytes=64)
+            pqs = work.tile([P, P], U8, name="pqs", align_bytes=64)
+            nc.vector.quantize_mx(
+                out=pq[:].bitcast(X4), scales=pqs[:],
+                in_=state["pg", n][:].rearrange("p n j -> p (n j)"),
+            )
+            state["pq", n] = (pq, pqs)
+
+        def v_mm(i):
+            b, ch = divmod(i, TILES)
+            ps = psum.tile([P, PACK, P], F32, name="quad_ps")
+            dcols = slice(P * ch, P * (ch + 1))
+            for t in range(PACK):
+                cols = slice(P * t, P * (t + 1))
+                nc.tensor.matmul_mx(
+                    out=ps[:, t, :], lhsT=xq[b][:, cols].bitcast(X4), lhsT_scale=xs[b][:, cols],
+                    rhs=wv_sb[:, dcols].bitcast(X4), rhs_scale=wvs_sb[:, dcols], start=True, stop=True,
+                )
+            state["vps", i] = ps
+
+        def v_gain(i):
+            b, ch = divmod(i, TILES)
+            m = P // PACK
+            nc.vector.tensor_tensor(
+                out=vg[b][:].rearrange("p (d m) t -> p d m t", d=PACK)[:, :, m * ch : m * (ch + 1), :],
+                in0=state["vps", i][:].rearrange("p t (m d) -> p d m t", d=PACK),
+                in1=u_bf[:].unsqueeze(1).unsqueeze(1).to_broadcast([P, PACK, m, PACK]),
+                op=ALU.mult,
+            )
+
+        def v_quant(b):
+            nc.vector.quantize_mx(
+                out=vq[b][:].bitcast(X4), scales=vs[b][:], in_=vg[b][:].rearrange("p n j -> p (n j)")
+            )
+
+        def out_mm(n):
+            b = n // TILES
+            pq, pqs = state["pq", n]
+            qd = psum.tile([P, PACK, P], F32, name="quad_ps")
+            for d in range(PACK):
+                cols = slice(P * d, P * (d + 1))
+                nc.tensor.matmul_mx(
+                    out=qd[:, d, :], lhsT=vq[b][:, cols].bitcast(X4), lhsT_scale=vs[b][:, cols],
+                    rhs=pq[:].bitcast(X4), rhs_scale=pqs[:], start=True, stop=True,
+                )
+            nat = psum.tile([P, D], F32, name="nat_ps", bufs=1)
+            nc.tensor.matmul_mx(
+                out=nat[:], lhsT=pq[:].bitcast(X4), lhsT_scale=pqs[:],
+                rhs=vq[b][:].bitcast(X4), rhs_scale=vs[b][:], start=True, stop=True,
+            )
+            state["qd", n], state["nat", n] = qd, nat
+
+        def nat_evac(n, eng):
+            b, t = divmod(n, TILES)
+            ob = work.tile([P, D], F32, name="ob")
+            src = state["nat", n][:].rearrange("p (d m) -> p m d", d=PACK)
+            dst = ob[:].rearrange("p (m d) -> p m d", d=PACK)
+            if eng == "s":
+                nc.scalar.copy(out=dst, in_=src)
+            else:
+                nc.vector.tensor_copy(out=dst, in_=src)
+            nc.sync.dma_start(
+                out=out_0[b].rearrange("(p t) d -> p t d", t=TILES)[:, t, :], in_=ob[:]
+            )
+
+        def quad_evac(n, p0, p1):
+            b, t = divmod(n, TILES)
+            nc.scalar.copy(
+                out=og[b][:].rearrange("m (p t) d -> m t p d", t=TILES)[:, t, p0:p1, :],
+                in_=state["qd", n][:].rearrange("m d p -> m p d")[:, p0:p1, :],
+            )
+
+        def o_quant(b, i0, i1):
+            nc.vector.quantize_mx(
+                out=oq[b][:, i0:i1].bitcast(X4), scales=os_[b][:, i0:i1],
+                in_=og[b][:, i0:i1, :].rearrange("m i d -> m (i d)"),
+            )
+            nc.sync.dma_start(
+                out=out_1[0][:, S * b + i0 : S * b + i1, :].rearrange("m i d -> m (i d)").bitcast(I32),
+                in_=oq[b][:, i0:i1].bitcast(I32),
+            )
+
+        def o_scales(b):
+            for q in range(4):
+                nc.sync.dma_start(
+                    out=out_2[0, 4 * q : 4 * q + 4, S * b : S * (b + 1)].bitcast(I32),
+                    in_=os_[b][32 * q : 32 * q + 4, :].bitcast(I32),
+                )
+
+        V_CHUNKS = {1: [0, 1], 2: [2, 3], 3: [4], 4: [5], 5: [6], 6: [7]}
+        X_AHEAD = {2: [4, 5, 6, 7]}
+        LAST = N_TILES - 1
+
+        def live(n):
+            return 0 <= n < N_TILES
+
+        def body():
+            x_turn(0)
+            x_quant(0)
+            syn(0)
+            rnd_mix(0)
+            for k in range(N_TILES):
+                if live(k - 3):
+                    out_mm(k - 3)
+                if live(k - 2):
+                    p_turn(k - 2)
+                logit(k)
+                if live(k - 1):
+                    recip(k - 1)
+                if live(k - 2):
+                    p_evac(k - 2)
+                if live(k - 3):
+                    quad_evac(k - 3, 0, P)
+                    if k < LAST:
+                        nat_evac(k - 3, "s")
+                for n in X_AHEAD.get(k, []):
+                    x_quant(n)
+                if k == 0:
+                    for n in range(1, TILES):
+                        x_turn(n)
+                        x_quant(n)
+                    for t in range(1, TILES):
+                        rnd_mix(t)
+                    nc.tensor.matmul(c_ps[:], lhsT=ones[:], rhs=c_row[:], start=True, stop=True)
+                for j, i in enumerate(V_CHUNKS.get(k, [])):
+                    if j > 0:
+                        v_mm(i)
+                    v_gain(i)
+                    if i % TILES == TILES - 1:
+                        v_quant(i // TILES)
+                row_max(k)
+                expo(k)
+                if live(k - 2):
+                    p_quant(k - 2)
+                if live(k - 1):
+                    pc(k - 1)
+                if live(k + 1):
+                    syn(k + 1)
+                for n in X_AHEAD.get(k + 1, []):
+                    x_turn(n)
+                for i in V_CHUNKS.get(k + 1, [])[:1]:
+                    v_mm(i)
+            nat_evac(LAST - 3, "v")
+            p_turn(LAST - 1)
+            recip(LAST)
+            out_mm(LAST - 2)
+            p_evac(LAST - 1)
+            o_quant(0, 0, S)
+            o_scales(0)
+            pc(LAST)
+            quad_evac(LAST - 2, 0, P)
+            p_turn(LAST)
+            p_quant(LAST - 1)
+            p_evac(LAST)
+            nat_evac(LAST - 2, "v")
+            out_mm(LAST - 1)
+            p_quant(LAST)
+            quad_evac(LAST - 1, 0, P)
+            nat_evac(LAST - 1, "v")
+            out_mm(LAST)
+            quad_evac(LAST, 0, P // 2)
+            quad_evac(LAST, P // 2, P)
+            o_quant(1, 0, S // 2)
+            o_quant(1, S // 2, S)
+            o_scales(1)
+            nat_evac(LAST, "s")
+
+        if MANUAL_ORDER:
+            ctx.enter_context(tc.manual_schedule())
+        body()

@@ -40,6 +40,7 @@ def tile_mixturedenserandomsynthesizer_x2_kernel(
         rnd_sb = keep.tile([P, TILES, S], BF16, name="rnd_sb")
         rm = keep.tile([P, TILES, S], F32, name="rm")
         mix_bf = keep.tile([P, 2], BF16, name="mix_bf")
+        mix_f = keep.tile([P, 2], F32, name="mix_f")
         u_bf = keep.tile([P, TILES], BF16, name="u_bf")
         c_row = keep.tile([P, S], BF16, name="c_row")
         ones = keep.tile([P, P], BF16, name="ones")
@@ -49,45 +50,50 @@ def tile_mixturedenserandomsynthesizer_x2_kernel(
         x_v = [x[b].rearrange("(p t) f -> p t f", t=TILES) for b in range(B)]
         rnd_v = rnd.rearrange("(p t) k -> p t k", t=TILES)
 
-        make_identity(nc, ident[:])
-        nc.gpsimd.dma_start(out=mix_bf[:], in_=mix.partition_broadcast(P))
         nc.vector.memset(ws_sb[:].bitcast(I32), 0)
         nc.vector.memset(wvs_sb[:].bitcast(I32), 0)
         nc.vector.memset(warm[:], 0.0)
         nc.vector.memset(c_row[:], 0.0)
         nc.vector.memset(ones[:], 1.0)
+        make_identity(nc, ident[:])
 
-        def load_scales(eng, dst, src):
+        def load_scales(dst, src):
             for q in range(4):
-                eng.dma_start(
+                nc.sync.dma_start(
                     out=dst[32 * q : 32 * q + 4, :].bitcast(I32),
                     in_=src[0, 4 * q : 4 * q + 4, :].bitcast(I32),
                 )
 
-        nc.sync.dma_start(out=x_sb[0][:, 0:1, :], in_=x_v[0][:, 0:1, :])
-        nc.sync.dma_start(
-            out=w_sb[:].bitcast(I32), in_=w_words[0].rearrange("p n t -> p (n t)").bitcast(I32)
-        )
-        load_scales(nc.scalar, ws_sb, w_scales)
+        def load_words(dst, src):
+            nc.sync.dma_start(
+                out=dst[:].bitcast(I32), in_=src[0].rearrange("p n t -> p (n t)").bitcast(I32)
+            )
+
+        nc.scalar.dma_start(out=mix_bf[:], in_=mix.partition_broadcast(P))
         nc.scalar.activation(out=warm[:], in_=warm[:], func=ACT.Exp)
-        nc.sync.dma_start(out=rnd_sb[:, 0:2, :], in_=rnd_v[:, 0:2, :])
+        nc.sync.dma_start(out=x_sb[0][:, 0:1, :], in_=x_v[0][:, 0:1, :])
+        load_scales(ws_sb, w_scales)
+        load_words(w_sb, w_words)
         nc.sync.dma_start(out=x_sb[0][:, 1:4, :], in_=x_v[0][:, 1:4, :])
+        nc.gpsimd.dma_start(out=rnd_sb[:, 0:2, :], in_=rnd_v[:, 0:2, :])
         nc.gpsimd.dma_start(out=c_row[0:1, :], in_=c.rearrange("(o k) -> o k", o=1))
         nc.gpsimd.dma_start(out=u_bf[:], in_=u.rearrange("(p t) -> p t", t=TILES))
-        nc.sync.dma_start(
-            out=wv_sb[:].bitcast(I32), in_=wv_words[0].rearrange("p n t -> p (n t)").bitcast(I32)
-        )
-        load_scales(nc.sync, wvs_sb, wv_scales)
+        load_scales(wvs_sb, wv_scales)
+        load_words(wv_sb, wv_words)
         nc.sync.dma_start(out=rnd_sb[:, 2:4, :], in_=rnd_v[:, 2:4, :])
         nc.sync.dma_start(out=x_sb[1][:], in_=x_v[1])
 
         c_ps = psum.tile([P, S], F32, name="c_ps", bufs=1)
 
-        def rnd_mix(t):
-            (nc.vector if t == 0 else nc.gpsimd).tensor_scalar(
-                out=rm[:, t, :], in0=rnd_sb[:, t, :], scalar1=mix_bf[:, 1:2], scalar2=0.0,
-                op0=ALU.mult, op1=ALU.add,
-            )
+        def rnd_mix(t, eng):
+            if eng == "v":
+                nc.vector.tensor_scalar(
+                    out=rm[:, t, :], in0=rnd_sb[:, t, :], scalar1=mix_f[:, 1:2], scalar2=None, op0=ALU.mult
+                )
+            else:
+                nc.scalar.activation(
+                    out=rm[:, t, :], in_=rnd_sb[:, t, :], func=ACT.Copy, scale=mix_f[:, 1:2]
+                )
 
         xq = [keep.tile([P, S], U32, name="xq%d" % b, align_bytes=64) for b in range(B)]
         xs = [keep.tile([P, S], U8, name="xs%d" % b, align_bytes=64) for b in range(B)]
@@ -135,7 +141,7 @@ def tile_mixturedenserandomsynthesizer_x2_kernel(
             t = n % TILES
             lg = work.tile([P, S], F32, name="lg")
             nc.vector.scalar_tensor_tensor(
-                out=lg[:], in0=state["syn", n][:], scalar=mix_bf[:, 0:1], in1=rm[:, t, :],
+                out=lg[:], in0=state["syn", n][:], scalar=mix_f[:, 0:1], in1=rm[:, t, :],
                 op0=ALU.mult, op1=ALU.add,
             )
             state["lg", n] = lg
@@ -230,7 +236,10 @@ def tile_mixturedenserandomsynthesizer_x2_kernel(
                     out=qd[:, d, :], lhsT=vq[b][:, cols].bitcast(X4), lhsT_scale=vs[b][:, cols],
                     rhs=pq[:].bitcast(X4), rhs_scale=pqs[:], start=True, stop=True,
                 )
-            nat = psum.tile([P, D], F32, name="nat_ps", bufs=1)
+            if n < N_TILES - 2:
+                nat = psum.tile([P, D], F32, name="nat_ps", bufs=1)
+            else:
+                nat = psum.tile([P, D], F32, name="syn_ps")
             nc.tensor.matmul_mx(
                 out=nat[:], lhsT=pq[:].bitcast(X4), lhsT_scale=pqs[:],
                 rhs=vq[b][:].bitcast(X4), rhs_scale=vs[b][:], start=True, stop=True,
@@ -238,21 +247,30 @@ def tile_mixturedenserandomsynthesizer_x2_kernel(
             state["qd", n], state["nat", n] = qd, nat
 
         def nat_evac(n, eng):
-            b, t = divmod(n, TILES)
-            ob = work.tile([P, D], F32, name="ob")
+            t = n % TILES
+            if n == N_TILES - 2:
+                ob = state["ob", n - 1]
+            else:
+                ob = work.tile([P, 2, D], F32, name="ob")
+            state["ob", n] = ob
+            half = 1 if n == N_TILES - 2 else 0
             src = state["nat", n][:].rearrange("p (d m) -> p m d", d=PACK)
-            dst = ob[:].rearrange("p (m d) -> p m d", d=PACK)
+            dst = ob[:, half, :].rearrange("p (m d) -> p m d", d=PACK)
             if eng == "s":
                 nc.scalar.copy(out=dst, in_=src)
             else:
                 nc.vector.tensor_copy(out=dst, in_=src)
-            nc.sync.dma_start(
-                out=out_0[b].rearrange("(p t) d -> p t d", t=TILES)[:, t, :], in_=ob[:]
+
+        def nat_store(n0, count, eng):
+            b, t = divmod(n0, TILES)
+            eng.dma_start(
+                out=out_0[b].rearrange("(p t) d -> p t d", t=TILES)[:, t : t + count, :],
+                in_=state["ob", n0][:, 0:count, :],
             )
 
-        def quad_evac(n, p0, p1):
+        def quad_evac(n, p0, p1, eng):
             b, t = divmod(n, TILES)
-            nc.scalar.copy(
+            (nc.scalar.copy if eng == "s" else nc.vector.tensor_copy)(
                 out=og[b][:].rearrange("m (p t) d -> m t p d", t=TILES)[:, t, p0:p1, :],
                 in_=state["qd", n][:].rearrange("m d p -> m p d")[:, p0:p1, :],
             )
@@ -284,73 +302,82 @@ def tile_mixturedenserandomsynthesizer_x2_kernel(
         def body():
             x_turn(0)
             x_quant(0)
+            nc.vector.tensor_copy(out=mix_f[:], in_=mix_bf[:])
             syn(0)
-            rnd_mix(0)
-            for k in range(N_TILES):
-                if live(k - 3):
-                    out_mm(k - 3)
+            rnd_mix(0, "v")
+            logit(0)
+            for n in range(1, TILES):
+                x_turn(n)
+            nc.tensor.matmul(c_ps[:], lhsT=ones[:], rhs=c_row[:], start=True, stop=True)
+            rnd_mix(1, "v")
+            x_quant(1)
+            syn(1)
+            row_max(0)
+            expo(0)
+            rnd_mix(2, "s")
+            rnd_mix(3, "s")
+            x_quant(2)
+            x_quant(3)
+            v_mm(0)
+            for k in range(1, N_TILES):
                 if live(k - 2):
                     p_turn(k - 2)
+                if live(k - 3):
+                    out_mm(k - 3)
                 logit(k)
-                if live(k - 1):
-                    recip(k - 1)
+                recip(k - 1)
                 if live(k - 2):
                     p_evac(k - 2)
                 if live(k - 3):
-                    quad_evac(k - 3, 0, P)
-                    if k < LAST:
-                        nat_evac(k - 3, "s")
+                    quad_evac(k - 3, 0, P, "s")
                 for n in X_AHEAD.get(k, []):
                     x_quant(n)
-                if k == 0:
-                    for n in range(1, TILES):
-                        x_turn(n)
-                        x_quant(n)
-                    for t in range(1, TILES):
-                        rnd_mix(t)
-                    nc.tensor.matmul(c_ps[:], lhsT=ones[:], rhs=c_row[:], start=True, stop=True)
                 for j, i in enumerate(V_CHUNKS.get(k, [])):
                     if j > 0:
                         v_mm(i)
                     v_gain(i)
                     if i % TILES == TILES - 1:
                         v_quant(i // TILES)
+                if k == LAST:
+                    o_quant(0, 0, S)
+                    o_scales(0)
                 row_max(k)
                 expo(k)
+                if live(k - 3):
+                    nat_evac(k - 3, "s")
+                    nat_store(k - 3, 1, nc.sync)
                 if live(k - 2):
                     p_quant(k - 2)
-                if live(k - 1):
-                    pc(k - 1)
+                pc(k - 1)
                 if live(k + 1):
                     syn(k + 1)
                 for n in X_AHEAD.get(k + 1, []):
                     x_turn(n)
                 for i in V_CHUNKS.get(k + 1, [])[:1]:
                     v_mm(i)
-            nat_evac(LAST - 3, "v")
             p_turn(LAST - 1)
             recip(LAST)
-            out_mm(LAST - 2)
             p_evac(LAST - 1)
-            o_quant(0, 0, S)
-            o_scales(0)
             pc(LAST)
-            quad_evac(LAST - 2, 0, P)
+            out_mm(LAST - 2)
             p_turn(LAST)
             p_quant(LAST - 1)
             p_evac(LAST)
-            nat_evac(LAST - 2, "v")
+            quad_evac(LAST - 2, 0, P, "v")
             out_mm(LAST - 1)
             p_quant(LAST)
-            quad_evac(LAST - 1, 0, P)
-            nat_evac(LAST - 1, "v")
+            quad_evac(LAST - 1, 0, P, "s")
+            nat_evac(LAST - 2, "v")
             out_mm(LAST)
-            quad_evac(LAST, 0, P // 2)
-            quad_evac(LAST, P // 2, P)
+            nat_evac(LAST - 1, "v")
+            nat_store(LAST - 2, 2, nc.sync)
+            quad_evac(LAST, 0, P // 2, "s")
+            quad_evac(LAST, P // 2, P, "s")
             o_quant(1, 0, S // 2)
             o_quant(1, S // 2, S)
             o_scales(1)
             nat_evac(LAST, "s")
+            nat_store(LAST, 1, nc.scalar)
 
         if MANUAL_ORDER:
             ctx.enter_context(tc.manual_schedule())

@@ -43,6 +43,8 @@ def tile_mixturedenserandomsynthesizer_x2_kernel(
         mix_f = keep.tile([P, 2], F32, name="mix_f")
         u_bf = keep.tile([P, TILES], BF16, name="u_bf")
         c_row = keep.tile([P, S], BF16, name="c_row")
+        u_f = keep.tile([P, TILES], F32, name="u_f")
+        vn = keep.tile([P, PACK, D], BF16, name="vn", align_bytes=64)
         ones = keep.tile([P, P], BF16, name="ones")
         ident = keep.tile([P, P], F32, name="ident")
         warm = keep.tile([P, 1], F32, name="warm")
@@ -71,11 +73,12 @@ def tile_mixturedenserandomsynthesizer_x2_kernel(
 
         nc.scalar.dma_start(out=mix_bf[:], in_=mix.partition_broadcast(P))
         nc.scalar.activation(out=warm[:], in_=warm[:], func=ACT.Exp)
-        nc.sync.dma_start(out=x_sb[0][:, 0:1, :], in_=x_v[0][:, 0:1, :])
+        nc.sync.dma_start(out=x_sb[0][:, 0:2, :], in_=x_v[0][:, 0:2, :])
         load_scales(ws_sb, w_scales)
+        nc.sync.dma_start(out=rnd_sb[:, 0:1, :], in_=rnd_v[:, 0:1, :])
         load_words(w_sb, w_words)
-        nc.sync.dma_start(out=x_sb[0][:, 1:4, :], in_=x_v[0][:, 1:4, :])
-        nc.gpsimd.dma_start(out=rnd_sb[:, 0:2, :], in_=rnd_v[:, 0:2, :])
+        nc.sync.dma_start(out=x_sb[0][:, 2:4, :], in_=x_v[0][:, 2:4, :])
+        nc.gpsimd.dma_start(out=rnd_sb[:, 1:2, :], in_=rnd_v[:, 1:2, :])
         nc.gpsimd.dma_start(out=c_row[0:1, :], in_=c.rearrange("(o k) -> o k", o=1))
         nc.gpsimd.dma_start(out=u_bf[:], in_=u.rearrange("(p t) -> p t", t=TILES))
         load_scales(wvs_sb, wv_scales)
@@ -221,6 +224,22 @@ def tile_mixturedenserandomsynthesizer_x2_kernel(
                 op=ALU.mult,
             )
 
+        def v0_slot(t):
+            cols = slice(P * t, P * (t + 1))
+            ps = psum.tile([P, D], F32, name="quad_ps")
+            nc.tensor.matmul_mx(
+                out=ps[:], lhsT=xq[0][:, cols].bitcast(X4), lhsT_scale=xs[0][:, cols],
+                rhs=wv_sb[:].bitcast(X4), rhs_scale=wvs_sb[:], start=True, stop=True,
+            )
+            nc.scalar.activation(
+                out=vn[:, t, :].rearrange("p (d m) -> p d m", d=PACK),
+                in_=ps[:].rearrange("p (m d) -> p d m", d=PACK),
+                func=ACT.Copy, scale=u_f[:, t : t + 1],
+            )
+
+        def v0_pack():
+            nc.vector.tensor_copy(out=vg[0][:], in_=vn[:].rearrange("p t n -> p n t"))
+
         def v_quant(b):
             nc.vector.quantize_mx(
                 out=vq[b][:].bitcast(X4), scales=vs[b][:], in_=vg[b][:].rearrange("p n j -> p (n j)")
@@ -236,7 +255,7 @@ def tile_mixturedenserandomsynthesizer_x2_kernel(
                     out=qd[:, d, :], lhsT=vq[b][:, cols].bitcast(X4), lhsT_scale=vs[b][:, cols],
                     rhs=pq[:].bitcast(X4), rhs_scale=pqs[:], start=True, stop=True,
                 )
-            if n < N_TILES - 2:
+            if n < N_TILES - 3 or n == N_TILES - 2:
                 nat = psum.tile([P, D], F32, name="nat_ps", bufs=1)
             else:
                 nat = psum.tile([P, D], F32, name="syn_ps")
@@ -247,26 +266,18 @@ def tile_mixturedenserandomsynthesizer_x2_kernel(
             state["qd", n], state["nat", n] = qd, nat
 
         def nat_evac(n, eng):
-            t = n % TILES
-            if n == N_TILES - 2:
-                ob = state["ob", n - 1]
-            else:
-                ob = work.tile([P, 2, D], F32, name="ob")
+            ob = work.tile([P, D], F32, name="ob")
             state["ob", n] = ob
-            half = 1 if n == N_TILES - 2 else 0
             src = state["nat", n][:].rearrange("p (d m) -> p m d", d=PACK)
-            dst = ob[:, half, :].rearrange("p (m d) -> p m d", d=PACK)
+            dst = ob[:].rearrange("p (m d) -> p m d", d=PACK)
             if eng == "s":
                 nc.scalar.copy(out=dst, in_=src)
             else:
                 nc.vector.tensor_copy(out=dst, in_=src)
 
-        def nat_store(n0, count, eng):
-            b, t = divmod(n0, TILES)
-            eng.dma_start(
-                out=out_0[b].rearrange("(p t) d -> p t d", t=TILES)[:, t : t + count, :],
-                in_=state["ob", n0][:, 0:count, :],
-            )
+        def nat_store(n, eng):
+            b, t = divmod(n, TILES)
+            eng.dma_start(out=out_0[b].rearrange("(p t) d -> p t d", t=TILES)[:, t, :], in_=state["ob", n][:])
 
         def quad_evac(n, p0, p1, eng):
             b, t = divmod(n, TILES)
@@ -280,20 +291,20 @@ def tile_mixturedenserandomsynthesizer_x2_kernel(
                 out=oq[b][:, i0:i1].bitcast(X4), scales=os_[b][:, i0:i1],
                 in_=og[b][:, i0:i1, :].rearrange("m i d -> m (i d)"),
             )
-            nc.sync.dma_start(
-                out=out_1[0][:, S * b + i0 : S * b + i1, :].rearrange("m i d -> m (i d)").bitcast(I32),
-                in_=oq[b][:, i0:i1].bitcast(I32),
-            )
 
         def o_scales(b):
+            nc.sync.dma_start(
+                out=out_1[0][:, S * b : S * (b + 1), :].rearrange("m i d -> m (i d)").bitcast(I32),
+                in_=oq[b][:].bitcast(I32),
+            )
             for q in range(4):
                 nc.sync.dma_start(
                     out=out_2[0, 4 * q : 4 * q + 4, S * b : S * (b + 1)].bitcast(I32),
                     in_=os_[b][32 * q : 32 * q + 4, :].bitcast(I32),
                 )
 
-        V_CHUNKS = {1: [0, 1], 2: [2, 3], 3: [4], 4: [5], 5: [6], 6: [7]}
-        X_AHEAD = {2: [4, 5, 6, 7]}
+        V_CHUNKS = {4: [4], 5: [5], 6: [6, 7]}
+        X_AHEAD = {3: [4, 5, 6, 7]}
         LAST = N_TILES - 1
 
         def live(n):
@@ -301,24 +312,25 @@ def tile_mixturedenserandomsynthesizer_x2_kernel(
 
         def body():
             x_turn(0)
-            x_quant(0)
+            x_turn(1)
             nc.vector.tensor_copy(out=mix_f[:], in_=mix_bf[:])
+            rnd_mix(1, "s")
+            x_quant(0)
             syn(0)
-            rnd_mix(0, "v")
-            logit(0)
-            for n in range(1, TILES):
-                x_turn(n)
-            nc.tensor.matmul(c_ps[:], lhsT=ones[:], rhs=c_row[:], start=True, stop=True)
-            rnd_mix(1, "v")
             x_quant(1)
             syn(1)
+            rnd_mix(0, "v")
+            logit(0)
+            x_turn(2)
+            x_turn(3)
+            nc.tensor.matmul(c_ps[:], lhsT=ones[:], rhs=c_row[:], start=True, stop=True)
             row_max(0)
             expo(0)
-            rnd_mix(2, "s")
-            rnd_mix(3, "s")
             x_quant(2)
             x_quant(3)
-            v_mm(0)
+            nc.vector.tensor_copy(out=u_f[:], in_=u_bf[:])
+            v0_slot(0)
+            v0_slot(1)
             for k in range(1, N_TILES):
                 if live(k - 2):
                     p_turn(k - 2)
@@ -332,34 +344,47 @@ def tile_mixturedenserandomsynthesizer_x2_kernel(
                     quad_evac(k - 3, 0, P, "s")
                 for n in X_AHEAD.get(k, []):
                     x_quant(n)
-                for j, i in enumerate(V_CHUNKS.get(k, [])):
-                    if j > 0:
-                        v_mm(i)
+                for i in V_CHUNKS.get(k, [])[:1]:
                     v_gain(i)
-                    if i % TILES == TILES - 1:
-                        v_quant(i // TILES)
+                if k == 1:
+                    rnd_mix(2, "v")
+                if k == 2:
+                    rnd_mix(3, "v")
+                    v0_pack()
                 if k == LAST:
                     o_quant(0, 0, S)
                     o_scales(0)
                 row_max(k)
                 expo(k)
+                for i in V_CHUNKS.get(k, [])[1:]:
+                    v_mm(i)
+                    v_gain(i)
+                if k == 2:
+                    v_quant(0)
                 if live(k - 3):
                     nat_evac(k - 3, "s")
-                    nat_store(k - 3, 1, nc.sync)
+                    nat_store(k - 3, nc.sync)
                 if live(k - 2):
                     p_quant(k - 2)
                 pc(k - 1)
+                if k == LAST - 1:
+                    v_quant(1)
                 if live(k + 1):
                     syn(k + 1)
+                if k == 1:
+                    v0_slot(2)
+                    v0_slot(3)
                 for n in X_AHEAD.get(k + 1, []):
                     x_turn(n)
                 for i in V_CHUNKS.get(k + 1, [])[:1]:
                     v_mm(i)
+            out_mm(LAST - 2)
             p_turn(LAST - 1)
             recip(LAST)
             p_evac(LAST - 1)
+            nat_evac(LAST - 2, "s")
+            nat_store(LAST - 2, nc.sync)
             pc(LAST)
-            out_mm(LAST - 2)
             p_turn(LAST)
             p_quant(LAST - 1)
             p_evac(LAST)
@@ -367,17 +392,16 @@ def tile_mixturedenserandomsynthesizer_x2_kernel(
             out_mm(LAST - 1)
             p_quant(LAST)
             quad_evac(LAST - 1, 0, P, "s")
-            nat_evac(LAST - 2, "v")
-            out_mm(LAST)
             nat_evac(LAST - 1, "v")
-            nat_store(LAST - 2, 2, nc.sync)
+            nat_store(LAST - 1, nc.sync)
+            out_mm(LAST)
             quad_evac(LAST, 0, P // 2, "s")
             quad_evac(LAST, P // 2, P, "s")
             o_quant(1, 0, S // 2)
             o_quant(1, S // 2, S)
             o_scales(1)
             nat_evac(LAST, "s")
-            nat_store(LAST, 1, nc.scalar)
+            nat_store(LAST, nc.scalar)
 
         if MANUAL_ORDER:
             ctx.enter_context(tc.manual_schedule())

@@ -79,8 +79,8 @@ def tile_mixturedenserandomsynthesizer_x2_kernel(
         load_words(w_sb, w_words)
         nc.sync.dma_start(out=x_sb[0][:, 2:4, :], in_=x_v[0][:, 2:4, :])
         nc.gpsimd.dma_start(out=rnd_sb[:, 1:2, :], in_=rnd_v[:, 1:2, :])
-        nc.gpsimd.dma_start(out=c_row[0:1, :], in_=c.rearrange("(o k) -> o k", o=1))
         nc.gpsimd.dma_start(out=u_bf[:], in_=u.rearrange("(p t) -> p t", t=TILES))
+        nc.gpsimd.dma_start(out=c_row[0:1, :], in_=c.rearrange("(o k) -> o k", o=1))
         load_scales(wvs_sb, wv_scales)
         load_words(wv_sb, wv_words)
         nc.sync.dma_start(out=rnd_sb[:, 2:4, :], in_=rnd_v[:, 2:4, :])
@@ -238,31 +238,43 @@ def tile_mixturedenserandomsynthesizer_x2_kernel(
             )
 
         def v0_pack():
-            nc.vector.tensor_copy(out=vg[0][:], in_=vn[:].rearrange("p t n -> p n t"))
+            nc.vector.tensor_copy(
+                out=vg[0][:].rearrange("p (c i) t -> p c t i", i=PACK),
+                in_=vn[:].rearrange("p t (c i) -> p c t i", i=PACK),
+            )
 
         def v_quant(b):
             nc.vector.quantize_mx(
                 out=vq[b][:].bitcast(X4), scales=vs[b][:], in_=vg[b][:].rearrange("p n j -> p (n j)")
             )
 
+        def nat_mm(nat, n):
+            b = n // TILES
+            pq, pqs = state["pq", n]
+            nc.tensor.matmul_mx(
+                out=nat[:], lhsT=pq[:].bitcast(X4), lhsT_scale=pqs[:],
+                rhs=vq[b][:].bitcast(X4), rhs_scale=vs[b][:], start=True, stop=True,
+            )
+
         def out_mm(n):
             b = n // TILES
             pq, pqs = state["pq", n]
             qd = psum.tile([P, PACK, P], F32, name="quad_ps")
+            if n == N_TILES - 1:
+                nat = psum.tile([P, D], F32, name="syn_ps")
+                nat_mm(nat, n)
             for d in range(PACK):
                 cols = slice(P * d, P * (d + 1))
                 nc.tensor.matmul_mx(
                     out=qd[:, d, :], lhsT=vq[b][:, cols].bitcast(X4), lhsT_scale=vs[b][:, cols],
                     rhs=pq[:].bitcast(X4), rhs_scale=pqs[:], start=True, stop=True,
                 )
-            if n < N_TILES - 3 or n == N_TILES - 2:
-                nat = psum.tile([P, D], F32, name="nat_ps", bufs=1)
-            else:
-                nat = psum.tile([P, D], F32, name="syn_ps")
-            nc.tensor.matmul_mx(
-                out=nat[:], lhsT=pq[:].bitcast(X4), lhsT_scale=pqs[:],
-                rhs=vq[b][:].bitcast(X4), rhs_scale=vs[b][:], start=True, stop=True,
-            )
+            if n < N_TILES - 1:
+                if n == N_TILES - 3:
+                    nat = psum.tile([P, D], F32, name="syn_ps")
+                else:
+                    nat = psum.tile([P, D], F32, name="nat_ps", bufs=1)
+                nat_mm(nat, n)
             state["qd", n], state["nat", n] = qd, nat
 
         def nat_evac(n, eng):
@@ -292,11 +304,13 @@ def tile_mixturedenserandomsynthesizer_x2_kernel(
                 in_=og[b][:, i0:i1, :].rearrange("m i d -> m (i d)"),
             )
 
-        def o_scales(b):
+        def o_store(b, i0, i1):
             nc.sync.dma_start(
-                out=out_1[0][:, S * b : S * (b + 1), :].rearrange("m i d -> m (i d)").bitcast(I32),
-                in_=oq[b][:].bitcast(I32),
+                out=out_1[0][:, S * b + i0 : S * b + i1, :].rearrange("m i d -> m (i d)").bitcast(I32),
+                in_=oq[b][:, i0:i1].bitcast(I32),
             )
+
+        def o_scales(b):
             for q in range(4):
                 nc.sync.dma_start(
                     out=out_2[0, 4 * q : 4 * q + 4, S * b : S * (b + 1)].bitcast(I32),
@@ -317,13 +331,12 @@ def tile_mixturedenserandomsynthesizer_x2_kernel(
             rnd_mix(1, "s")
             x_quant(0)
             syn(0)
+            rnd_mix(0, "v")
             x_quant(1)
             syn(1)
-            rnd_mix(0, "v")
             logit(0)
             x_turn(2)
             x_turn(3)
-            nc.tensor.matmul(c_ps[:], lhsT=ones[:], rhs=c_row[:], start=True, stop=True)
             row_max(0)
             expo(0)
             x_quant(2)
@@ -331,6 +344,7 @@ def tile_mixturedenserandomsynthesizer_x2_kernel(
             nc.vector.tensor_copy(out=u_f[:], in_=u_bf[:])
             v0_slot(0)
             v0_slot(1)
+            nc.tensor.matmul(c_ps[:], lhsT=ones[:], rhs=c_row[:], start=True, stop=True)
             for k in range(1, N_TILES):
                 if live(k - 2):
                     p_turn(k - 2)
@@ -350,22 +364,25 @@ def tile_mixturedenserandomsynthesizer_x2_kernel(
                     rnd_mix(2, "v")
                 if k == 2:
                     rnd_mix(3, "v")
-                    v0_pack()
                 if k == LAST:
-                    o_quant(0, 0, S)
-                    o_scales(0)
+                    p_quant(k - 2)
+                    pc(k - 1)
                 row_max(k)
                 expo(k)
+                if k == 2:
+                    v0_pack()
                 for i in V_CHUNKS.get(k, [])[1:]:
                     v_mm(i)
                     v_gain(i)
-                if k == 2:
-                    v_quant(0)
+                if k == LAST:
+                    break
                 if live(k - 3):
                     nat_evac(k - 3, "s")
                     nat_store(k - 3, nc.sync)
                 if live(k - 2):
                     p_quant(k - 2)
+                if k == 2:
+                    v_quant(0)
                 pc(k - 1)
                 if k == LAST - 1:
                     v_quant(1)
@@ -378,30 +395,37 @@ def tile_mixturedenserandomsynthesizer_x2_kernel(
                     x_turn(n)
                 for i in V_CHUNKS.get(k + 1, [])[:1]:
                     v_mm(i)
-            out_mm(LAST - 2)
             p_turn(LAST - 1)
+            out_mm(LAST - 2)
+            o_quant(0, 0, S)
+            o_store(0, 0, S)
+            o_scales(0)
             recip(LAST)
             p_evac(LAST - 1)
+            pc(LAST)
+            nat_evac(LAST - 3, "s")
+            nat_store(LAST - 3, nc.sync)
             nat_evac(LAST - 2, "s")
             nat_store(LAST - 2, nc.sync)
-            pc(LAST)
             p_turn(LAST)
             p_quant(LAST - 1)
+            out_mm(LAST - 1)
             p_evac(LAST)
             quad_evac(LAST - 2, 0, P, "v")
-            out_mm(LAST - 1)
             p_quant(LAST)
             quad_evac(LAST - 1, 0, P, "s")
+            out_mm(LAST)
             nat_evac(LAST - 1, "v")
             nat_store(LAST - 1, nc.sync)
-            out_mm(LAST)
+            nat_evac(LAST, "v")
+            nat_store(LAST, nc.sync)
             quad_evac(LAST, 0, P // 2, "s")
             quad_evac(LAST, P // 2, P, "s")
             o_quant(1, 0, S // 2)
+            o_store(1, 0, S // 2)
             o_quant(1, S // 2, S)
+            o_store(1, S // 2, S)
             o_scales(1)
-            nat_evac(LAST, "s")
-            nat_store(LAST, nc.scalar)
 
         if MANUAL_ORDER:
             ctx.enter_context(tc.manual_schedule())

from contextlib import ExitStack

import concourse.mybir as mybir
from concourse.masks import make_identity

B, S, D = 2, 512, 512
FLOPS = 3 * 2 * B * S * S * D

F32 = mybir.dt.float32
BF16 = mybir.dt.bfloat16
U32 = mybir.dt.uint32
I32 = mybir.dt.int32
U8 = mybir.dt.uint8
X4 = mybir.dt.float8_e4m3fn_x4
ALU = mybir.AluOpType
ACT = mybir.ActivationFunctionType
AXIS = mybir.AxisListType

P = 128
PACK = 4
TILES = S // P
N_TILES = B * TILES
MANUAL_ORDER = True


def tile_mixturedenserandomsynthesizer_x2_kernel(
    tc, x, w_words, w_scales, rnd, mix, wv_words, wv_scales, c, u, out_0, out_1, out_2
):
    nc = tc.nc
    with ExitStack() as ctx:
        keep = ctx.enter_context(tc.tile_pool(name="keep", bufs=1))
        work = ctx.enter_context(tc.tile_pool(name="work", bufs=4))
        psum = ctx.enter_context(tc.psum_pool(name="psum", bufs=2))

        x_sb = [keep.tile([P, TILES, D], BF16, name="x_sb%d" % b) for b in range(B)]
        w_sb = keep.tile([P, S], U32, name="w_sb", align_bytes=64)
        wv_sb = keep.tile([P, D], U32, name="wv_sb", align_bytes=64)
        ws_sb = keep.tile([P, S], U8, name="ws_sb", align_bytes=64)
        wvs_sb = keep.tile([P, D], U8, name="wvs_sb", align_bytes=64)
        rnd_sb = keep.tile([P, TILES, S], BF16, name="rnd_sb")
        rm = keep.tile([P, TILES, S], F32, name="rm")
        mix_bf = keep.tile([P, 2], BF16, name="mix_bf")
        mix_f = keep.tile([P, 2], F32, name="mix_f")
        u_bf = keep.tile([P, TILES], BF16, name="u_bf")
        c_row = keep.tile([P, S], BF16, name="c_row")
        u_f = keep.tile([P, TILES], F32, name="u_f")
        vn = keep.tile([P, PACK, D], BF16, name="vn", align_bytes=64)
        ones = keep.tile([P, P], BF16, name="ones")
        ident = keep.tile([P, P], F32, name="ident")
        warm = keep.tile([P, 1], F32, name="warm")

        x_v = [x[b].rearrange("(p t) f -> p t f", t=TILES) for b in range(B)]
        rnd_v = rnd.rearrange("(p t) k -> p t k", t=TILES)

        nc.vector.memset(ws_sb[:].bitcast(I32), 0)
        nc.vector.memset(wvs_sb[:].bitcast(I32), 0)
        nc.vector.memset(warm[:], 0.0)
        nc.vector.memset(c_row[:], 0.0)
        nc.vector.memset(ones[:], 1.0)
        make_identity(nc, ident[:])

        def load_scales(dst, src):
            for q in range(4):
                nc.sync.dma_start(
                    out=dst[32 * q : 32 * q + 4, :].bitcast(I32),
                    in_=src[0, 4 * q : 4 * q + 4, :].bitcast(I32),
                )

        def load_words(dst, src):
            nc.sync.dma_start(
                out=dst[:].bitcast(I32), in_=src[0].rearrange("p n t -> p (n t)").bitcast(I32)
            )

        nc.scalar.dma_start(out=mix_bf[:], in_=mix.partition_broadcast(P))
        nc.scalar.activation(out=warm[:], in_=warm[:], func=ACT.Exp)
        nc.sync.dma_start(out=x_sb[0][:, 0:2, :], in_=x_v[0][:, 0:2, :])
        load_scales(ws_sb, w_scales)
        nc.sync.dma_start(out=rnd_sb[:, 0:1, :], in_=rnd_v[:, 0:1, :])
        load_words(w_sb, w_words)
        nc.sync.dma_start(out=x_sb[0][:, 2:4, :], in_=x_v[0][:, 2:4, :])
        nc.gpsimd.dma_start(out=rnd_sb[:, 1:2, :], in_=rnd_v[:, 1:2, :])
        nc.gpsimd.dma_start(out=u_bf[:], in_=u.rearrange("(p t) -> p t", t=TILES))
        nc.gpsimd.dma_start(out=c_row[0:1, :], in_=c.rearrange("(o k) -> o k", o=1))
        load_scales(wvs_sb, wv_scales)
        load_words(wv_sb, wv_words)
        nc.sync.dma_start(out=rnd_sb[:, 2:4, :], in_=rnd_v[:, 2:4, :])
        nc.sync.dma_start(out=x_sb[1][:], in_=x_v[1])

        c_ps = psum.tile([P, S], F32, name="c_ps", bufs=1)

        def rnd_mix(t, eng):
            if eng == "v":
                nc.vector.tensor_scalar(
                    out=rm[:, t, :], in0=rnd_sb[:, t, :], scalar1=mix_f[:, 1:2], scalar2=None, op0=ALU.mult
                )
            else:
                nc.scalar.activation(
                    out=rm[:, t, :], in_=rnd_sb[:, t, :], func=ACT.Copy, scale=mix_f[:, 1:2]
                )

        xq = [keep.tile([P, S], U32, name="xq%d" % b, align_bytes=64) for b in range(B)]
        xs = [keep.tile([P, S], U8, name="xs%d" % b, align_bytes=64) for b in range(B)]
        vg = [keep.tile([P, D, PACK], BF16, name="vg%d" % b, align_bytes=64) for b in range(B)]
        vq = [keep.tile([P, D], U32, name="vq%d" % b, align_bytes=64) for b in range(B)]
        vs = [keep.tile([P, D], U8, name="vs%d" % b, align_bytes=64) for b in range(B)]
        og = [keep.tile([P, S, PACK], BF16, name="og%d" % b, align_bytes=64) for b in range(B)]
        oq = [keep.tile([P, S], U32, name="oq%d" % b, align_bytes=64) for b in range(B)]
        os_ = [keep.tile([P, S], U8, name="os%d" % b, align_bytes=64) for b in range(B)]

        state = {}

        def x_turn(n):
            b, t = divmod(n, TILES)
            words = x_sb[b][:, t, :].bitcast(F32)
            xt = psum.tile([P, 2, P], F32, name="turn")
            for h in range(2):
                nc.tensor.transpose(xt[:, h, :], words[:, h : 2 * P : 2], ident[:])
            xg = work.tile([P, P, PACK], BF16, name="xg", align_bytes=64)
            nc.scalar.copy(
                out=xg[:].rearrange("p n j -> p (n j)").bitcast(F32).rearrange("p (n h) -> p n h", h=2),
                in_=xt[:].rearrange("p h n -> p n h"),
            )
            state["xg", n] = xg

        def x_quant(n):
            b, t = divmod(n, TILES)
            cols = slice(P * t, P * (t + 1))
            nc.vector.quantize_mx(
                out=xq[b][:, cols].bitcast(X4), scales=xs[b][:, cols],
                in_=state["xg", n][:].rearrange("p n j -> p (n j)"),
            )

        def syn(n):
            b, t = divmod(n, TILES)
            cols = slice(P * t, P * (t + 1))
            ps = psum.tile([P, S], F32, name="syn_ps")
            nc.tensor.matmul_mx(
                out=ps[:], lhsT=xq[b][:, cols].bitcast(X4), lhsT_scale=xs[b][:, cols],
                rhs=w_sb[:].bitcast(X4), rhs_scale=ws_sb[:], start=True, stop=True,
            )
            state["syn", n] = ps

        def logit(n):
            t = n % TILES
            lg = work.tile([P, S], F32, name="lg")
            nc.vector.scalar_tensor_tensor(
                out=lg[:], in0=state["syn", n][:], scalar=mix_f[:, 0:1], in1=rm[:, t, :],
                op0=ALU.mult, op1=ALU.add,
            )
            state["lg", n] = lg

        def row_max(n):
            nmax = work.tile([P, 1], F32, name="nmax")
            nc.vector.tensor_reduce(
                out=nmax[:], in_=state["lg", n][:], axis=AXIS.X, op=ALU.max, negate=True
            )
            state["nmax", n] = nmax

        def expo(n):
            e = work.tile([P, S], F32, name="e")
            tot = work.tile([P, 1], F32, name="tot")
            nc.scalar.activation(
                out=e[:], in_=state["lg", n][:], func=ACT.Exp, bias=state["nmax", n][:],
                scale=1.0, accum_out=tot[:],
            )
            state["e", n], state["tot", n] = e, tot

        def recip(n):
            rinv = work.tile([P, 1], F32, name="rinv")
            nc.vector.reciprocal(rinv[:], state["tot", n][:])
            state["rinv", n] = rinv

        def pc(n):
            pcs = work.tile([P, S], BF16, name="pcs", align_bytes=64)
            nc.vector.scalar_tensor_tensor(
                out=pcs[:], in0=state["e", n][:], scalar=state["rinv", n][:], in1=c_ps[:],
                op0=ALU.mult, op1=ALU.mult,
            )
            state["pcs", n] = pcs

        def p_turn(n):
            words = state["pcs", n][:].bitcast(F32)
            pt = psum.tile([P, 2, P], F32, name="turn")
            for h in range(2):
                nc.tensor.transpose(pt[:, h, :], words[:, h : 2 * P : 2], ident[:])
            state["pt", n] = pt

        def p_evac(n):
            pg = work.tile([P, P, PACK], BF16, name="pg", align_bytes=64)
            nc.scalar.copy(
                out=pg[:].rearrange("p n j -> p (n j)").bitcast(F32).rearrange("p (n h) -> p n h", h=2),
                in_=state["pt", n][:].rearrange("p h n -> p n h"),
            )
            state["pg", n] = pg

        def p_quant(n):
            pq = work.tile([P, P], U32, name="pq", align_bytes=64)
            pqs = work.tile([P, P], U8, name="pqs", align_bytes=64)
            nc.vector.quantize_mx(
                out=pq[:].bitcast(X4), scales=pqs[:],
                in_=state["pg", n][:].rearrange("p n j -> p (n j)"),
            )
            state["pq", n] = (pq, pqs)

        def v_mm(i):
            b, ch = divmod(i, TILES)
            ps = psum.tile([P, PACK, P], F32, name="quad_ps")
            dcols = slice(P * ch, P * (ch + 1))
            for t in range(PACK):
                cols = slice(P * t, P * (t + 1))
                nc.tensor.matmul_mx(
                    out=ps[:, t, :], lhsT=xq[b][:, cols].bitcast(X4), lhsT_scale=xs[b][:, cols],
                    rhs=wv_sb[:, dcols].bitcast(X4), rhs_scale=wvs_sb[:, dcols], start=True, stop=True,
                )
            state["vps", i] = ps

        def v_gain(i):
            b, ch = divmod(i, TILES)
            m = P // PACK
            nc.vector.tensor_tensor(
                out=vg[b][:].rearrange("p (d m) t -> p d m t", d=PACK)[:, :, m * ch : m * (ch + 1), :],
                in0=state["vps", i][:].rearrange("p t (m d) -> p d m t", d=PACK),
                in1=u_bf[:].unsqueeze(1).unsqueeze(1).to_broadcast([P, PACK, m, PACK]),
                op=ALU.mult,
            )

        def v0_slot(t):
            cols = slice(P * t, P * (t + 1))
            ps = psum.tile([P, D], F32, name="quad_ps")
            nc.tensor.matmul_mx(
                out=ps[:], lhsT=xq[0][:, cols].bitcast(X4), lhsT_scale=xs[0][:, cols],
                rhs=wv_sb[:].bitcast(X4), rhs_scale=wvs_sb[:], start=True, stop=True,
            )
            nc.scalar.activation(
                out=vn[:, t, :].rearrange("p (d m) -> p d m", d=PACK),
                in_=ps[:].rearrange("p (m d) -> p d m", d=PACK),
                func=ACT.Copy, scale=u_f[:, t : t + 1],
            )

        def v0_pack():
            nc.vector.tensor_copy(
                out=vg[0][:].rearrange("p (c i) t -> p c t i", i=PACK),
                in_=vn[:].rearrange("p t (c i) -> p c t i", i=PACK),
            )

        def v_quant(b):
            nc.vector.quantize_mx(
                out=vq[b][:].bitcast(X4), scales=vs[b][:], in_=vg[b][:].rearrange("p n j -> p (n j)")
            )

        def nat_mm(nat, n):
            b = n // TILES
            pq, pqs = state["pq", n]
            nc.tensor.matmul_mx(
                out=nat[:], lhsT=pq[:].bitcast(X4), lhsT_scale=pqs[:],
                rhs=vq[b][:].bitcast(X4), rhs_scale=vs[b][:], start=True, stop=True,
            )

        def out_mm(n):
            b = n // TILES
            pq, pqs = state["pq", n]
            qd = psum.tile([P, PACK, P], F32, name="quad_ps")
            if n == N_TILES - 1:
                nat = psum.tile([P, D], F32, name="syn_ps")
                nat_mm(nat, n)
            for d in range(PACK):
                cols = slice(P * d, P * (d + 1))
                nc.tensor.matmul_mx(
                    out=qd[:, d, :], lhsT=vq[b][:, cols].bitcast(X4), lhsT_scale=vs[b][:, cols],
                    rhs=pq[:].bitcast(X4), rhs_scale=pqs[:], start=True, stop=True,
                )
            if n < N_TILES - 1:
                if n == N_TILES - 3:
                    nat = psum.tile([P, D], F32, name="syn_ps")
                else:
                    nat = psum.tile([P, D], F32, name="nat_ps", bufs=1)
                nat_mm(nat, n)
            state["qd", n], state["nat", n] = qd, nat

        def nat_evac(n, eng):
            ob = work.tile([P, D], F32, name="ob")
            state["ob", n] = ob
            src = state["nat", n][:].rearrange("p (d m) -> p m d", d=PACK)
            dst = ob[:].rearrange("p (m d) -> p m d", d=PACK)
            if eng == "s":
                nc.scalar.copy(out=dst, in_=src)
            else:
                nc.vector.tensor_copy(out=dst, in_=src)

        def nat_store(n, eng):
            b, t = divmod(n, TILES)
            eng.dma_start(out=out_0[b].rearrange("(p t) d -> p t d", t=TILES)[:, t, :], in_=state["ob", n][:])

        def quad_evac(n, p0, p1, eng):
            b, t = divmod(n, TILES)
            (nc.scalar.copy if eng == "s" else nc.vector.tensor_copy)(
                out=og[b][:].rearrange("m (p t) d -> m t p d", t=TILES)[:, t, p0:p1, :],
                in_=state["qd", n][:].rearrange("m d p -> m p d")[:, p0:p1, :],
            )

        def o_quant(b, i0, i1):
            nc.vector.quantize_mx(
                out=oq[b][:, i0:i1].bitcast(X4), scales=os_[b][:, i0:i1],
                in_=og[b][:, i0:i1, :].rearrange("m i d -> m (i d)"),
            )

        def o_store(b, i0, i1):
            nc.sync.dma_start(
                out=out_1[0][:, S * b + i0 : S * b + i1, :].rearrange("m i d -> m (i d)").bitcast(I32),
                in_=oq[b][:, i0:i1].bitcast(I32),
            )

        def o_scales(b):
            for q in range(4):
                nc.sync.dma_start(
                    out=out_2[0, 4 * q : 4 * q + 4, S * b : S * (b + 1)].bitcast(I32),
                    in_=os_[b][32 * q : 32 * q + 4, :].bitcast(I32),
                )

        V_CHUNKS = {4: [4], 5: [5], 6: [6, 7]}
        X_AHEAD = {3: [4, 5, 6, 7]}
        LAST = N_TILES - 1

        def live(n):
            return 0 <= n < N_TILES

        def body():
            x_turn(0)
            x_turn(1)
            nc.vector.tensor_copy(out=mix_f[:], in_=mix_bf[:])
            rnd_mix(1, "s")
            x_quant(0)
            syn(0)
            rnd_mix(0, "v")
            x_quant(1)
            syn(1)
            logit(0)
            x_turn(2)
            x_turn(3)
            row_max(0)
            expo(0)
            x_quant(2)
            x_quant(3)
            nc.vector.tensor_copy(out=u_f[:], in_=u_bf[:])
            v0_slot(0)
            v0_slot(1)
            nc.tensor.matmul(c_ps[:], lhsT=ones[:], rhs=c_row[:], start=True, stop=True)
            for k in range(1, N_TILES):
                if live(k - 2):
                    p_turn(k - 2)
                if live(k - 3):
                    out_mm(k - 3)
                logit(k)
                recip(k - 1)
                if live(k - 2):
                    p_evac(k - 2)
                if live(k - 3):
                    quad_evac(k - 3, 0, P, "s")
                for n in X_AHEAD.get(k, []):
                    x_quant(n)
                for i in V_CHUNKS.get(k, [])[:1]:
                    v_gain(i)
                if k == 1:
                    rnd_mix(2, "v")
                if k == 2:
                    rnd_mix(3, "v")
                if k == LAST:
                    p_quant(k - 2)
                    pc(k - 1)
                row_max(k)
                expo(k)
                if k == 2:
                    v0_pack()
                for i in V_CHUNKS.get(k, [])[1:]:
                    v_mm(i)
                    v_gain(i)
                if k == LAST:
                    break
                if live(k - 3):
                    nat_evac(k - 3, "s")
                    nat_store(k - 3, nc.sync)
                if live(k - 2):
                    p_quant(k - 2)
                if k == 2:
                    v_quant(0)
                pc(k - 1)
                if k == LAST - 1:
                    v_quant(1)
                if live(k + 1):
                    syn(k + 1)
                if k == 1:
                    v0_slot(2)
                    v0_slot(3)
                for n in X_AHEAD.get(k + 1, []):
                    x_turn(n)
                for i in V_CHUNKS.get(k + 1, [])[:1]:
                    v_mm(i)
            p_turn(LAST - 1)
            out_mm(LAST - 2)
            o_quant(0, 0, S)
            o_store(0, 0, S)
            o_scales(0)
            recip(LAST)
            p_evac(LAST - 1)
            pc(LAST)
            nat_evac(LAST - 3, "s")
            nat_store(LAST - 3, nc.sync)
            nat_evac(LAST - 2, "s")
            nat_store(LAST - 2, nc.sync)
            p_turn(LAST)
            p_quant(LAST - 1)
            out_mm(LAST - 1)
            p_evac(LAST)
            quad_evac(LAST - 2, 0, P, "v")
            p_quant(LAST)
            quad_evac(LAST - 1, 0, P, "s")
            out_mm(LAST)
            nat_evac(LAST - 1, "v")
            nat_store(LAST - 1, nc.sync)
            nat_evac(LAST, "v")
            nat_store(LAST, nc.sync)
            quad_evac(LAST, 0, P // 2, "s")
            quad_evac(LAST, P // 2, P, "s")
            o_quant(1, 0, S // 2)
            o_store(1, 0, S // 2)
            o_quant(1, S // 2, S)
            o_store(1, S // 2, S)
            o_scales(1)

        if MANUAL_ORDER:
            ctx.enter_context(tc.manual_schedule())
        body()
